import numpy as np
import ml_dtypes


def mxq(x, axis, fmt="e4m3"):
    dtype, down = {"e4m3": (ml_dtypes.float8_e4m3fn, 7), "e5m2": (ml_dtypes.float8_e5m2, 14)}[fmt]
    v = np.moveaxis(np.asarray(x, np.float32).astype(ml_dtypes.bfloat16).astype(np.float64), axis, -1)
    blocks = v.reshape(v.shape[:-1] + (-1, 32))
    amax = np.abs(blocks).max(-1, keepdims=True)
    byte = np.maximum(np.where(amax > 0, np.frexp(amax)[1] - 1 + 127, 0) - down, 1)
    scale = np.exp2(byte - 127.0)
    codes = (blocks / scale).astype(np.float32).astype(dtype).astype(np.float64)
    return np.moveaxis((codes * scale).reshape(v.shape), -1, axis)


WIDE = False


def mx_kscale(k):
    if not WIDE:
        return np.ones(k)
    levels = np.array([10, -10, 5, -5, 0])
    if k % 512:
        return np.exp2(np.random.permutation(np.resize(levels, k // 32))).repeat(32)
    a = np.empty((k // 512, 16))
    for p in range(k // 512):
        a[p, :8] = np.random.permutation(np.resize(levels, 8))
        for g in range(8):
            far = levels[np.abs(levels - a[p, g]) >= 10]
            a[p, g + 8] = far[np.random.randint(len(far))]
    return np.exp2(a.ravel()).repeat(32)


def f64(x):
    return np.asarray(x).astype(np.float64)


def striped(idx):
    return np.tile(idx.reshape(-1, 16).T, (8, 1)).astype(np.uint16)


def unstriped(offs):
    return offs[:16].T.reshape(-1).astype(np.int64)


def striped8(idx):
    return np.concatenate([x.reshape(-1, 16).T for x in idx]).astype(np.uint16)


def runs(offs, k):
    lists = np.stack([offs[16 * r : 16 * r + 16].T.reshape(-1) for r in range(8)]).astype(np.int64)
    return lists[np.arange(k) % 512 // 64]


def pack_weight(w):
    k, n = w.shape
    w = f64(np.asarray(w, np.float32).astype(ml_dtypes.bfloat16)).reshape(k // 32, 32, n)
    amax = np.abs(w).max(1)
    byte = np.clip(np.where(amax > 0, np.frexp(amax)[1] - 1 + 127 - 7, 1), 1, 254)
    scaled = (w * np.exp2(127.0 - byte)[:, None, :]).reshape(k, n).astype(np.float32)
    words = np.ascontiguousarray(scaled.reshape(k // 512, 128, 4, n).transpose(0, 1, 3, 2)).astype(ml_dtypes.float8_e4m3fn).view(np.uint8)
    return words, np.ascontiguousarray(byte.astype(np.uint8).reshape(k // 512, 16, n))


def unpack_weight(words, scales):
    g, p, n, _ = words.shape
    vals = np.ascontiguousarray(words).view(ml_dtypes.float8_e4m3fn).astype(np.float64) * np.repeat(np.exp2(scales.astype(np.float64) - 127.0), 8, axis=1)[..., None]
    return vals.transpose(0, 1, 3, 2).reshape(g * 512, n)


E2M1 = np.array([0.0, 0.5, 1.0, 1.5, 2.0, 3.0, 4.0, 6.0, -0.0, -0.5, -1.0, -1.5, -2.0, -3.0, -4.0, -6.0])


def pack_fp4(w):
    k, n = w.shape
    w = f64(np.asarray(w, np.float32).astype(ml_dtypes.bfloat16)).reshape(k // 32, 32, n)
    amax = np.abs(w).max(1)
    mant, ex = np.frexp(amax / 6.0)
    byte = np.clip(np.where(amax > 0, np.where(mant > 0.5, ex, ex - 1) + 127, 1), 1, 254)
    scaled = (w * np.exp2(127.0 - byte)[:, None, :]).reshape(k, n).astype(np.float32)
    c = np.ascontiguousarray(scaled.reshape(k // 512, 128, 4, n).transpose(0, 1, 3, 2)).astype(ml_dtypes.float4_e2m1fn).view(np.uint8) & 0xF
    words = (c[..., 0::2] | (c[..., 1::2] << 4)).reshape(k // 512, 128, 2 * n)
    return np.ascontiguousarray(words), np.ascontiguousarray(byte.astype(np.uint8).reshape(k // 512, 16, n))


def unpack_fp4(words, scales):
    g, _, n = scales.shape
    words = np.ascontiguousarray(words).reshape(g, 128, n, 2)
    nib = np.empty((g, 128, n, 4), np.uint8)
    nib[..., 0::2] = words & 0xF
    nib[..., 1::2] = words >> 4
    vals = E2M1[nib] * np.repeat(np.exp2(scales.astype(np.float64) - 127.0), 8, axis=1)[..., None]
    return vals.transpose(0, 1, 3, 2).reshape(g * 512, n)


def planes(y):
    n, m = y.shape
    v = y.astype(np.float32).astype(ml_dtypes.bfloat16).astype(np.float64).reshape(n // 32, 32, m)
    top = np.abs(v).max(1)
    byte = np.clip(np.where(top > 0, np.frexp(top)[1] - 1 + 127 - 7, 1), 1, 254)
    codes = (v * np.exp2(127.0 - byte)[:, None, :]).reshape(n, m).astype(np.float32).astype(ml_dtypes.float8_e4m3fn).view(np.uint8)
    words = codes.reshape(n // 512, 128, 4, m).transpose(0, 1, 3, 2)
    return np.ascontiguousarray(words), np.ascontiguousarray(byte.astype(np.uint8).reshape(n // 512, 16, m))


K, T, S, N, G, H = 512, 2048, 512, 512, 2048, 512


def setup_inputs():
    n = np.random.standard_normal
    s = mx_kscale(K)[:, None]
    u = mx_kscale(S)
    packed_xT = pack_weight(n((K, T)) * s)
    packed_dT = pack_weight(n((K, G)) / s)
    packed_w1 = pack_fp4(n((H, N)) / np.sqrt(H) / u[:, None])
    return {
        "x_words": packed_xT[0],
        "x_scales": packed_xT[1],
        "d_words": packed_dT[0],
        "d_scales": packed_dT[1],
        "gn": (np.random.uniform(0.5, 1.5, (H, 1)) * u[:, None]).astype(np.float32),
        "w1_words": packed_w1[0],
        "w1_scales": packed_w1[1],
        "offs": striped(np.random.permutation(T)[:S]),
        "k1": striped8(np.random.randint(0, G, (8, H))),
        "two": striped(np.random.permutation(T)[:S]),
        "n1": striped(np.random.permutation(S)),
        "n2": striped(np.random.permutation(S)),
        "n3": striped8(np.stack([np.random.permutation(S) for _ in range(8)])),
    }


def reference(x_words, x_scales, d_words, d_scales, gn, w1_words, w1_scales, offs, k1, two, n1, n2, n3):
    d_k1 = unpack_weight(d_words, d_scales)[np.arange(K)[:, None], runs(k1, K)]
    xq = unpack_weight(x_words, x_scales)[:, unstriped(offs)]
    a = 0.0625 * (d_k1.T @ xq)
    x_two = unpack_weight(x_words, x_scales)[:, unstriped(two)]
    b = 0.0625 * (d_k1.T @ x_two)
    z = f64(gn) * (a * (np.tanh(b[:, unstriped(n1)] - b[:, unstriped(n2)])))
    h = unpack_fp4(w1_words, w1_scales).T @ mxq(z, 0, "e4m3")
    pa = h[np.arange(N)[:, None], runs(n3, N)]
    out_0 = (2.0 * (h * pa)) / ((h) ** 2 + (pa) ** 2 + 0.5)
    return (out_0,) + planes(out_0)

@@ -1,0 +1,238 @@
+from contextlib import ExitStack
+
+import concourse.mybir as mybir
+
+F32 = mybir.dt.float32
+BF16 = mybir.dt.bfloat16
+I32 = mybir.dt.int32
+U32 = mybir.dt.uint32
+U16 = mybir.dt.uint16
+U8 = mybir.dt.uint8
+FP8X4 = mybir.dt.float8_e4m3fn_x4
+FP4X4 = mybir.dt.float4_e2m1fn_x4
+ACT = mybir.ActivationFunctionType
+ALU = mybir.AluOpType
+
+P = 128
+PACK = 4
+T = 2048
+S = 512
+ZW = 256
+OW = 128
+FLOPS = 3 * 2 * 512 * 512 * 512
+
+
+def tile_picked_twksjointbharm_none_po_kernel(
+    tc, x_words, x_scales, d_words, d_scales, gn, w1_words, w1_scales, offs, k1, two, n1, n2, n3, out_0, out_1, out_2
+):
+    nc = tc.nc
+    with ExitStack() as ctx:
+        keep = ctx.enter_context(tc.tile_pool(name="keep", bufs=1))
+        psum = ctx.enter_context(tc.psum_pool(name="psum", bufs=1))
+
+        def tile(name, shape, dtype):
+            return keep.tile(shape, dtype, name=name, align_bytes=64)
+
+        def load_list(name, src):
+            t = tile(name, [P, S // 16], U16)
+            nc.sync.dma_start(t[:], src)
+            return t
+
+        def words_view(src):
+            return src[0].rearrange("p n r -> p (n r)").bitcast(I32)
+
+        def entries(lst, start, count):
+            return lst[:, start // 16 : (start + count) // 16]
+
+        d_bytes = tile("d_bytes", [P, T], U8)
+        x_bytes = tile("x_bytes", [P, T], U8)
+        nc.vector.memset(d_bytes[:].bitcast(I32), 0)
+        nc.vector.memset(x_bytes[:].bitcast(I32), 0)
+        placed = tile("placed", [P, 2 * S], U8)
+        idx_scales = tile("idx_scales", [P, S], U8)
+        for t in (placed, idx_scales):
+            nc.vector.memset(t[:].bitcast(I32), 0)
+
+        k1_t = load_list("k1_t", k1)
+        nc.sync.dma_start(d_bytes[0:P:8, :].bitcast(I32), d_scales[0].bitcast(I32))
+        two_t = load_list("two_t", two)
+        nc.sync.dma_start(x_bytes[0:P:8, :].bitcast(I32), x_scales[0].bitcast(I32))
+        n1_t = load_list("n1_t", n1)
+        n2_t = load_list("n2_t", n2)
+        d_table = tile("d_table", [P, T], U32)
+        nc.sync.dma_start(d_table[:].bitcast(I32), words_view(d_words))
+        x_table = tile("x_table", [P, T], U32)
+        nc.sync.dma_start(x_table[:].bitcast(I32), words_view(x_words))
+        n3_t = load_list("n3_t", n3)
+        gain = tile("gain", [P, PACK], F32)
+        nc.sync.dma_start(gain[:], gn.rearrange("(p t) o -> p (t o)", t=PACK))
+        w_raw = tile("w_raw", [P, 2 * S], U8)
+        nc.sync.dma_start(w_raw[:].bitcast(I32), w1_words[0].bitcast(I32))
+        offs_t = load_list("offs_t", offs)
+
+        def deal(engine_copy, dst, src):
+            engine_copy(dst.rearrange("p (t m) -> p m t", t=PACK), src.rearrange("p (m t) -> p m t", t=PACK))
+
+        def place_rows(queue, dst, src):
+            for r in range(4):
+                queue.dma_start(dst[r:P:32, :].bitcast(I32), src[8 * r : P : 32, :].bitcast(I32))
+
+        staged = keep.tile([P, 2 * S], U8, name="staged", tag="byte_stage", align_bytes=64)
+        key_bytes = tile("key_bytes", [P, S], U8)
+        nc.vector.tensor_copy(key_bytes[:], d_bytes[:].indirect(k1_t[:]))
+        deal(nc.vector.tensor_copy, staged[:, :S], key_bytes[:])
+        two_bytes = tile("two_bytes", [P, S], U8)
+        nc.vector.tensor_copy(two_bytes[:], x_bytes[:].indirect(two_t[:]))
+        nc.vector.tensor_copy(staged[:, S:].bitcast(I32), two_bytes[:].bitcast(I32))
+        place_rows(nc.scalar, placed, staged)
+        key_words = keep.tile([P, S], U32, name="key_words", tag="word_stage", align_bytes=64)
+        nc.vector.tensor_copy(key_words[:], d_table[:].indirect(k1_t[:]))
+        key_codes = tile("key_codes", [P, S], U32)
+        deal(nc.vector.tensor_copy, key_codes[:], key_words[:])
+        two_codes = tile("two_codes", [P, S], U32)
+        nc.vector.tensor_copy(two_codes[:], x_table[:].indirect(two_t[:]))
+
+        def score(name, codes, scales):
+            banks = []
+            for t in range(PACK):
+                bank = psum.tile([P, S], F32, name=f"{name}{t}")
+                cols = slice(P * t, P * (t + 1))
+                nc.tensor.matmul_mx(
+                    out=bank[:], lhsT=key_codes[:, cols].bitcast(FP8X4), lhsT_scale=placed[:, cols],
+                    rhs=codes[:].bitcast(FP8X4), rhs_scale=scales, start=True, stop=True,
+                )
+                banks.append(bank)
+            return banks
+
+        b_banks = score("bh", two_codes, placed[:, S:])
+
+        idx_bytes = tile("idx_bytes", [P, S], U8)
+        nc.vector.tensor_copy(idx_bytes[:], x_bytes[:].indirect(offs_t[:]))
+        place_rows(nc.sync, idx_scales, idx_bytes)
+        idx_codes = tile("idx_codes", [P, S], U32)
+        nc.vector.tensor_copy(idx_codes[:], x_table[:].indirect(offs_t[:]))
+        a_banks = score("a", idx_codes, idx_scales[:])
+
+        w_bytes = keep.tile([P, S], U8, name="w_bytes", tag="word_stage", align_bytes=64)
+        nc.gpsimd.memset(w_bytes[:].bitcast(I32), 0)
+        for q in range(4):
+            nc.sync.dma_start(w_bytes[32 * q : 32 * q + 4, :].bitcast(I32), w1_scales[0, 4 * q : 4 * q + 4, :].bitcast(I32))
+        gain16 = tile("gain16", [P, PACK], F32)
+        nc.gpsimd.tensor_scalar(gain16[:], gain[:], 0.0625, 0.0, ALU.mult, ALU.add)
+        w_codes = keep.tile([P, 2 * S], U8, name="w_codes", tag="byte_stage", align_bytes=64)
+        deal(nc.scalar.copy, w_codes[:].bitcast(U16), w_raw[:].bitcast(U16))
+        w_scales = tile("w_scales", [P, S], U8)
+        deal(nc.vector.tensor_copy, w_scales[:], w_bytes[:])
+
+        b_rows = [tile(f"b_row{t}", [P, S], F32) for t in range(PACK)]
+        h_rows = [tile(f"h_row{t}", [P, S], F32) for t in range(PACK)]
+        h_sq = tile("h_sq", [P, PACK, S], F32)
+        halves = S // ZW
+        b1 = [tile(f"b1_{c}", [P, PACK, ZW], F32) for c in range(halves)]
+        diff = [tile(f"diff_{c}", [P, PACK, ZW], F32) for c in range(halves)]
+        th = [tile(f"th_{c}", [P, PACK, ZW], F32) for c in range(halves)]
+        z_rows = [tile(f"z_rows_{c}", [P, PACK, ZW], BF16) for c in range(halves)]
+        h_banks = {}
+
+        def fetch_b(c, t):
+            if c == 0:
+                nc.scalar.copy(b_rows[t][:], b_banks[t][:])
+            nc.scalar.activation(b1[c][:, t, :], b_rows[t][:].indirect(entries(n1_t, c * ZW, ZW)), ACT.Copy)
+            nc.vector.tensor_tensor(diff[c][:, t, :], b_rows[t][:].indirect(entries(n2_t, c * ZW, ZW)), b1[c][:, t, :], ALU.subtract)
+
+        def make_z(c, t):
+            nc.scalar.activation(th[c][:, t, :], diff[c][:, t, :], ACT.Tanh, scale=-0.0625)
+            nc.vector.scalar_tensor_tensor(
+                z_rows[c][:, t, :], a_banks[t][:, c * ZW : (c + 1) * ZW], gain16[:, t : t + 1], th[c][:, t, :], ALU.mult, ALU.mult
+            )
+
+        def layer(c):
+            cols = slice(c * ZW, (c + 1) * ZW)
+            z_packed = tile(f"z_packed_{c}", [P, ZW, PACK], BF16)
+            nc.vector.tensor_copy(z_packed[:], z_rows[c][:].rearrange("p t j -> p j t"))
+            z_codes = tile(f"z_codes_{c}", [P, ZW], U32)
+            z_scales = tile(f"z_scales_{c}", [P, ZW], U8)
+            nc.vector.quantize_mx(out=z_codes[:].bitcast(FP8X4), scales=z_scales[:], in_=z_packed[:].rearrange("p j t -> p (j t)"))
+            for u in range(2):
+                h_banks[c, u] = psum.tile([P, 2, ZW], F32, name=f"bh{2 * c + u}")
+            for t in range(PACK):
+                nc.tensor.matmul_mx(
+                    out=h_banks[c, t // 2][:, t % 2, :], lhsT=w_codes[:, 2 * P * t : 2 * P * (t + 1)].bitcast(FP4X4),
+                    lhsT_scale=w_scales[:, P * t : P * (t + 1)],
+                    rhs=z_codes[:].bitcast(FP8X4), rhs_scale=z_scales[:], start=True, stop=True,
+                )
+            for t in range(PACK):
+                nc.scalar.copy(h_rows[t][:, cols], h_banks[c, t // 2][:, t % 2, :])
+
+        def square_h(c):
+            for u in range(2):
+                nc.scalar.activation(h_sq[:, 2 * u : 2 * u + 2, c * ZW : (c + 1) * ZW], h_banks[c, u][:], ACT.Square)
+
+        steps = [(c, t) for c in range(halves) for t in range(PACK)]
+        for k in range(len(steps) + 2):
+            if k < len(steps):
+                fetch_b(*steps[k])
+            if k >= 2:
+                c, t = steps[k - 2]
+                make_z(c, t)
+                if t == PACK - 1:
+                    layer(c)
+                    if c < halves - 1:
+                        square_h(c)
+
+        y_codes = tile("y_codes", [P, S], U32)
+        y_scales = tile("y_scales", [P, S], U8)
+        out_rows = out_0.rearrange("(p t) j -> p t j", t=PACK)
+        out_words = words_view(out_1)
+        chunks = S // OW
+        pa = [tile(f"pa_{c}", [P, PACK, OW], F32) for c in range(chunks)]
+        pa_sq = [tile(f"pa_sq_{c}", [P, PACK, OW], F32) for c in range(chunks)]
+        num = [tile(f"num_{c}", [P, PACK, OW], F32) for c in range(chunks)]
+        den = [tile(f"den_{c}", [P, PACK, OW], F32) for c in range(chunks)]
+        inv = [tile(f"inv_{c}", [P, PACK, OW], F32) for c in range(chunks)]
+
+        def fetch_h(c):
+            for t in range(PACK):
+                looked_up = h_rows[t][:].indirect(entries(n3_t, c * OW, OW))
+                if t < PACK - 1:
+                    nc.vector.tensor_copy(pa[c][:, t, :], looked_up)
+                else:
+                    nc.scalar.activation(pa[c][:, t, :], looked_up, ACT.Copy)
+            nc.scalar.activation(pa_sq[c][:], pa[c][:], ACT.Square)
+
+        def sums(c):
+            cols = slice(c * OW, (c + 1) * OW)
+            nc.vector.scalar_tensor_tensor(den[c][:], pa_sq[c][:], 0.5, h_sq[:, :, cols], ALU.add, ALU.add)
+            for t in range(PACK):
+                nc.vector.tensor_tensor(num[c][:, t, :], h_rows[t][:, cols], pa[c][:, t, :], ALU.mult)
+
+        def invert(c):
+            root = tile(f"root_{c}", [P, PACK, OW], F32)
+            nc.scalar.activation(root[:], den[c][:], ACT.Abs_reciprocal_sqrt, scale=0.5)
+            nc.scalar.activation(inv[c][:], root[:], ACT.Square)
+
+        def finish(c):
+            cols = slice(c * OW, (c + 1) * OW)
+            y = tile(f"y_{c}", [P, PACK, OW], F32)
+            nc.vector.tensor_tensor(y[:], num[c][:], inv[c][:], ALU.mult)
+            nc.sync.dma_start(out_rows[:, :, cols], y[:])
+            y_packed = tile(f"y_packed_{c}", [P, OW, PACK], BF16)
+            nc.vector.tensor_copy(y_packed[:], y[:].rearrange("p t j -> p j t"))
+            nc.vector.quantize_mx(
+                out=y_codes[:, cols].bitcast(FP8X4), scales=y_scales[:, cols], in_=y_packed[:].rearrange("p j t -> p (j t)")
+            )
+            nc.sync.dma_start(out_words[:, cols], y_codes[:, cols].bitcast(I32))
+
+        for k in range(chunks + 2):
+            if k < chunks:
+                fetch_h(k)
+                if k == 0:
+                    square_h(halves - 1)
+                sums(k)
+            if 0 <= k - 1 < chunks:
+                invert(k - 1)
+            if 0 <= k - 2 < chunks:
+                finish(k - 2)
+        for q in range(4):
+            queue = nc.sync if q % 2 == 0 else nc.scalar
+            queue.dma_start(out_2[0, 4 * q : 4 * q + 4, :].bitcast(I32), y_scales[32 * q : 32 * q + 4, :].bitcast(I32))

@@ -19,6 +19,7 @@ T = 2048
 S = 512
 ZW = 256
 OW = 128
+ON_VECTOR = (2, 2, 3, 3)
 FLOPS = 3 * 2 * 512 * 512 * 512
 
 
@@ -46,29 +47,26 @@ def tile_picked_twksjointbharm_none_po_kernel(
 
         d_bytes = tile("d_bytes", [P, T], U8)
         x_bytes = tile("x_bytes", [P, T], U8)
+        key_scales = tile("key_scales", [P, S], U8)
+        w_bytes = tile("w_bytes", [P, S], U8)
         nc.vector.memset(d_bytes[:].bitcast(I32), 0)
-        nc.vector.memset(x_bytes[:].bitcast(I32), 0)
-        placed = tile("placed", [P, 2 * S], U8)
-        idx_scales = tile("idx_scales", [P, S], U8)
-        for t in (placed, idx_scales):
-            nc.vector.memset(t[:].bitcast(I32), 0)
+        nc.gpsimd.memset(x_bytes[:, : T // 2].bitcast(I32), 0)
+        nc.vector.memset(x_bytes[:, T // 2 :].bitcast(I32), 0)
+        nc.vector.memset(key_scales[:].bitcast(I32), 0)
+        nc.vector.memset(w_bytes[:].bitcast(I32), 0)
+
+        def load_scale_rows(dst, src):
+            for q in range(4):
+                nc.sync.dma_start(dst[32 * q : 32 * q + 4, :].bitcast(I32), src[0, 4 * q : 4 * q + 4, :].bitcast(I32))
 
         k1_t = load_list("k1_t", k1)
-        nc.sync.dma_start(d_bytes[0:P:8, :].bitcast(I32), d_scales[0].bitcast(I32))
         two_t = load_list("two_t", two)
-        nc.sync.dma_start(x_bytes[0:P:8, :].bitcast(I32), x_scales[0].bitcast(I32))
-        n1_t = load_list("n1_t", n1)
-        n2_t = load_list("n2_t", n2)
+        nc.sync.dma_start(d_bytes[0:P:8, :].bitcast(I32), d_scales[0].bitcast(I32))
         d_table = tile("d_table", [P, T], U32)
         nc.sync.dma_start(d_table[:].bitcast(I32), words_view(d_words))
+        load_scale_rows(x_bytes, x_scales)
         x_table = tile("x_table", [P, T], U32)
         nc.sync.dma_start(x_table[:].bitcast(I32), words_view(x_words))
-        n3_t = load_list("n3_t", n3)
-        gain = tile("gain", [P, PACK], F32)
-        nc.sync.dma_start(gain[:], gn.rearrange("(p t) o -> p (t o)", t=PACK))
-        w_raw = tile("w_raw", [P, 2 * S], U8)
-        nc.sync.dma_start(w_raw[:].bitcast(I32), w1_words[0].bitcast(I32))
-        offs_t = load_list("offs_t", offs)
 
         def deal(engine_copy, dst, src):
             engine_copy(dst.rearrange("p (t m) -> p m t", t=PACK), src.rearrange("p (m t) -> p m t", t=PACK))
@@ -77,19 +75,31 @@ def tile_picked_twksjointbharm_none_po_kernel(
             for r in range(4):
                 queue.dma_start(dst[r:P:32, :].bitcast(I32), src[8 * r : P : 32, :].bitcast(I32))
 
-        staged = keep.tile([P, 2 * S], U8, name="staged", tag="byte_stage", align_bytes=64)
         key_bytes = tile("key_bytes", [P, S], U8)
         nc.vector.tensor_copy(key_bytes[:], d_bytes[:].indirect(k1_t[:]))
-        deal(nc.vector.tensor_copy, staged[:, :S], key_bytes[:])
-        two_bytes = tile("two_bytes", [P, S], U8)
-        nc.vector.tensor_copy(two_bytes[:], x_bytes[:].indirect(two_t[:]))
-        nc.vector.tensor_copy(staged[:, S:].bitcast(I32), two_bytes[:].bitcast(I32))
-        place_rows(nc.scalar, placed, staged)
-        key_words = keep.tile([P, S], U32, name="key_words", tag="word_stage", align_bytes=64)
-        nc.vector.tensor_copy(key_words[:], d_table[:].indirect(k1_t[:]))
+        staged = tile("staged", [P, S], U8)
+        deal(nc.vector.tensor_copy, staged[:], key_bytes[:])
+        place_rows(nc.sync, key_scales, staged)
+        offs_t = load_list("offs_t", offs)
+        n1_t = load_list("n1_t", n1)
+        n2_t = load_list("n2_t", n2)
+        gain = tile("gain", [P, PACK], F32)
+        nc.sync.dma_start(gain[:], gn.rearrange("(p t) o -> p (t o)", t=PACK))
+        w_raw = tile("w_raw", [P, 2 * S], U8)
+        nc.sync.dma_start(w_raw[:].bitcast(I32), w1_words[0].bitcast(I32))
+        load_scale_rows(w_bytes, w1_scales)
+        n3_t = load_list("n3_t", n3)
         key_codes = tile("key_codes", [P, S], U32)
-        deal(nc.vector.tensor_copy, key_codes[:], key_words[:])
-        two_codes = tile("two_codes", [P, S], U32)
+        dealt_codes = key_codes[:].rearrange("p (t m) -> p m t", t=PACK)
+        key_words = []
+        for u in range(2):
+            key_words.append(keep.tile([P, S // 2], U32, name=f"key_words_{u}", tag=f"word_stage_{u}", align_bytes=64))
+            nc.vector.tensor_copy(key_words[u][:], d_table[:].indirect(entries(k1_t, u * S // 2, S // 2)))
+        for u in range(2):
+            nc.vector.tensor_copy(dealt_codes[:, u * P // 2 : (u + 1) * P // 2, :], key_words[u][:].rearrange("p (m t) -> p m t", t=PACK))
+        two_scales = tile("two_scales", [P, S], U8)
+        nc.vector.tensor_copy(two_scales[:], x_bytes[:].indirect(two_t[:]))
+        two_codes = keep.tile([P, S], U32, name="two_codes", tag="word_stage_0", align_bytes=64)
         nc.vector.tensor_copy(two_codes[:], x_table[:].indirect(two_t[:]))
 
         def score(name, codes, scales):
@@ -98,35 +108,30 @@ def tile_picked_twksjointbharm_none_po_kernel(
                 bank = psum.tile([P, S], F32, name=f"{name}{t}")
                 cols = slice(P * t, P * (t + 1))
                 nc.tensor.matmul_mx(
-                    out=bank[:], lhsT=key_codes[:, cols].bitcast(FP8X4), lhsT_scale=placed[:, cols],
+                    out=bank[:], lhsT=key_codes[:, cols].bitcast(FP8X4), lhsT_scale=key_scales[:, cols],
                     rhs=codes[:].bitcast(FP8X4), rhs_scale=scales, start=True, stop=True,
                 )
                 banks.append(bank)
             return banks
 
-        b_banks = score("bh", two_codes, placed[:, S:])
+        b_banks = score("bh", two_codes, two_scales[:])
 
-        idx_bytes = tile("idx_bytes", [P, S], U8)
-        nc.vector.tensor_copy(idx_bytes[:], x_bytes[:].indirect(offs_t[:]))
-        place_rows(nc.sync, idx_scales, idx_bytes)
-        idx_codes = tile("idx_codes", [P, S], U32)
+        idx_codes = keep.tile([P, S], U32, name="idx_codes", tag="word_stage_1", align_bytes=64)
         nc.vector.tensor_copy(idx_codes[:], x_table[:].indirect(offs_t[:]))
+        idx_scales = tile("idx_scales", [P, S], U8)
+        nc.vector.tensor_copy(idx_scales[:], x_bytes[:].indirect(offs_t[:]))
         a_banks = score("a", idx_codes, idx_scales[:])
 
-        w_bytes = keep.tile([P, S], U8, name="w_bytes", tag="word_stage", align_bytes=64)
-        nc.gpsimd.memset(w_bytes[:].bitcast(I32), 0)
-        for q in range(4):
-            nc.sync.dma_start(w_bytes[32 * q : 32 * q + 4, :].bitcast(I32), w1_scales[0, 4 * q : 4 * q + 4, :].bitcast(I32))
         gain16 = tile("gain16", [P, PACK], F32)
         nc.gpsimd.tensor_scalar(gain16[:], gain[:], 0.0625, 0.0, ALU.mult, ALU.add)
-        w_codes = keep.tile([P, 2 * S], U8, name="w_codes", tag="byte_stage", align_bytes=64)
+        w_codes = tile("w_codes", [P, 2 * S], U8)
         deal(nc.scalar.copy, w_codes[:].bitcast(U16), w_raw[:].bitcast(U16))
         w_scales = tile("w_scales", [P, S], U8)
         deal(nc.vector.tensor_copy, w_scales[:], w_bytes[:])
 
         b_rows = [tile(f"b_row{t}", [P, S], F32) for t in range(PACK)]
         h_rows = [tile(f"h_row{t}", [P, S], F32) for t in range(PACK)]
-        h_sq = tile("h_sq", [P, PACK, S], F32)
+        h_sq = {}
         halves = S // ZW
         b1 = [tile(f"b1_{c}", [P, PACK, ZW], F32) for c in range(halves)]
         diff = [tile(f"diff_{c}", [P, PACK, ZW], F32) for c in range(halves)]
@@ -138,7 +143,12 @@ def tile_picked_twksjointbharm_none_po_kernel(
             if c == 0:
                 nc.scalar.copy(b_rows[t][:], b_banks[t][:])
             nc.scalar.activation(b1[c][:, t, :], b_rows[t][:].indirect(entries(n1_t, c * ZW, ZW)), ACT.Copy)
-            nc.vector.tensor_tensor(diff[c][:, t, :], b_rows[t][:].indirect(entries(n2_t, c * ZW, ZW)), b1[c][:, t, :], ALU.subtract)
+            at_n2 = b_rows[t][:].indirect(entries(n2_t, c * ZW, ZW))
+            if (c, t) == steps[-1]:
+                b2 = tile("b2", [P, ZW], F32)
+                nc.scalar.activation(b2[:], at_n2, ACT.Copy)
+                at_n2 = b2[:]
+            nc.vector.tensor_tensor(diff[c][:, t, :], at_n2, b1[c][:, t, :], ALU.subtract)
 
         def make_z(c, t):
             nc.scalar.activation(th[c][:, t, :], diff[c][:, t, :], ACT.Tanh, scale=-0.0625)
@@ -148,7 +158,7 @@ def tile_picked_twksjointbharm_none_po_kernel(
 
         def layer(c):
             cols = slice(c * ZW, (c + 1) * ZW)
-            z_packed = tile(f"z_packed_{c}", [P, ZW, PACK], BF16)
+            z_packed = keep.tile([P, ZW, PACK], BF16, name=f"z_packed_{c}", tag=f"packed_{c}", align_bytes=64)
             nc.vector.tensor_copy(z_packed[:], z_rows[c][:].rearrange("p t j -> p j t"))
             z_codes = tile(f"z_codes_{c}", [P, ZW], U32)
             z_scales = tile(f"z_scales_{c}", [P, ZW], U8)
@@ -164,11 +174,7 @@ def tile_picked_twksjointbharm_none_po_kernel(
             for t in range(PACK):
                 nc.scalar.copy(h_rows[t][:, cols], h_banks[c, t // 2][:, t % 2, :])
 
-        def square_h(c):
-            for u in range(2):
-                nc.scalar.activation(h_sq[:, 2 * u : 2 * u + 2, c * ZW : (c + 1) * ZW], h_banks[c, u][:], ACT.Square)
-
-        steps = [(c, t) for c in range(halves) for t in range(PACK)]
+        steps = sorted(((c, t) for c in range(halves) for t in range(PACK)), key=lambda s: (2 * s[1] + 3 * s[0], s[0]))
         for k in range(len(steps) + 2):
             if k < len(steps):
                 fetch_b(*steps[k])
@@ -177,8 +183,14 @@ def tile_picked_twksjointbharm_none_po_kernel(
                 make_z(c, t)
                 if t == PACK - 1:
                     layer(c)
-                    if c < halves - 1:
-                        square_h(c)
+        h_sq[0] = keep.tile([P, PACK, ZW], F32, name="h_sq_0", tag="packed_1", align_bytes=64)
+        for t in range(PACK):
+            nc.vector.tensor_tensor(h_sq[0][:, t, :], h_rows[t][:, :ZW], h_rows[t][:, :ZW], ALU.mult)
+
+        def square_second_half():
+            h_sq[1] = tile("h_sq_1", [P, PACK, ZW], F32)
+            for u in range(2):
+                nc.scalar.activation(h_sq[1][:, 2 * u : 2 * u + 2, :], h_banks[1, u][:], ACT.Square)
 
         y_codes = tile("y_codes", [P, S], U32)
         y_scales = tile("y_scales", [P, S], U8)
@@ -194,17 +206,19 @@ def tile_picked_twksjointbharm_none_po_kernel(
         def fetch_h(c):
             for t in range(PACK):
                 looked_up = h_rows[t][:].indirect(entries(n3_t, c * OW, OW))
-                if t < PACK - 1:
+                if t < ON_VECTOR[c]:
                     nc.vector.tensor_copy(pa[c][:, t, :], looked_up)
                 else:
                     nc.scalar.activation(pa[c][:, t, :], looked_up, ACT.Copy)
             nc.scalar.activation(pa_sq[c][:], pa[c][:], ACT.Square)
 
         def sums(c):
-            cols = slice(c * OW, (c + 1) * OW)
-            nc.vector.scalar_tensor_tensor(den[c][:], pa_sq[c][:], 0.5, h_sq[:, :, cols], ALU.add, ALU.add)
-            for t in range(PACK):
-                nc.vector.tensor_tensor(num[c][:, t, :], h_rows[t][:, cols], pa[c][:, t, :], ALU.mult)
+            half, start = divmod(c * OW, ZW)
+            cols = slice(start, start + OW)
+            nc.vector.scalar_tensor_tensor(den[c][:], pa_sq[c][:], 0.5, h_sq[half][:, :, cols], ALU.add, ALU.add)
+            for u in range(2):
+                pair = slice(2 * u, 2 * u + 2)
+                nc.vector.tensor_tensor(num[c][:, pair, :], h_banks[half, u][:, :, cols], pa[c][:, pair, :], ALU.mult)
 
         def invert(c):
             root = tile(f"root_{c}", [P, PACK, OW], F32)
@@ -223,16 +237,17 @@ def tile_picked_twksjointbharm_none_po_kernel(
             )
             nc.sync.dma_start(out_words[:, cols], y_codes[:, cols].bitcast(I32))
 
-        for k in range(chunks + 2):
+        for k in range(chunks + 3):
             if k < chunks:
                 fetch_h(k)
-                if k == 0:
-                    square_h(halves - 1)
-                sums(k)
+            if k == 2:
+                square_second_half()
             if 0 <= k - 1 < chunks:
-                invert(k - 1)
+                sums(k - 1)
             if 0 <= k - 2 < chunks:
-                finish(k - 2)
+                invert(k - 2)
+            if 0 <= k - 3 < chunks:
+                finish(k - 3)
         for q in range(4):
             queue = nc.sync if q % 2 == 0 else nc.scalar
             queue.dma_start(out_2[0, 4 * q : 4 * q + 4, :].bitcast(I32), y_scales[32 * q : 32 * q + 4, :].bitcast(I32))

@@ -181,6 +181,9 @@ def tile_picked_twksjointbharm_none_po_kernel(
             if k >= 2:
                 c, t = steps[k - 2]
                 make_z(c, t)
+                if k == len(steps) + 1:
+                    warm = tile("warm", [P, 1], F32)
+                    nc.scalar.activation(warm[:], th[c][:, t, 0:1], ACT.Abs_reciprocal_sqrt, bias=2.0)
                 if t == PACK - 1:
                     layer(c)
         h_sq[0] = keep.tile([P, PACK, ZW], F32, name="h_sq_0", tag="packed_1", align_bytes=64)

@@ -141,13 +141,10 @@ def tile_picked_twksjointbharm_none_po_kernel(
 
         def fetch_b(c, t):
             if c == 0:
-                nc.scalar.copy(b_rows[t][:], b_banks[t][:])
+                copy_out = nc.vector.tensor_copy if t == PACK - 1 else nc.scalar.copy
+                copy_out(b_rows[t][:], b_banks[t][:])
             nc.scalar.activation(b1[c][:, t, :], b_rows[t][:].indirect(entries(n1_t, c * ZW, ZW)), ACT.Copy)
             at_n2 = b_rows[t][:].indirect(entries(n2_t, c * ZW, ZW))
-            if (c, t) == steps[-1]:
-                b2 = tile("b2", [P, ZW], F32)
-                nc.scalar.activation(b2[:], at_n2, ACT.Copy)
-                at_n2 = b2[:]
             nc.vector.tensor_tensor(diff[c][:, t, :], at_n2, b1[c][:, t, :], ALU.subtract)
 
         def make_z(c, t):
@@ -223,21 +220,33 @@ def tile_picked_twksjointbharm_none_po_kernel(
                 pair = slice(2 * u, 2 * u + 2)
                 nc.vector.tensor_tensor(num[c][:, pair, :], h_banks[half, u][:, :, cols], pa[c][:, pair, :], ALU.mult)
 
+        def pieces(c):
+            count = 2 if c >= chunks - 2 else 1
+            return [slice(i * OW // count, (i + 1) * OW // count) for i in range(count)]
+
         def invert(c):
             root = tile(f"root_{c}", [P, PACK, OW], F32)
-            nc.scalar.activation(root[:], den[c][:], ACT.Abs_reciprocal_sqrt, scale=0.5)
-            nc.scalar.activation(inv[c][:], root[:], ACT.Square)
+            for part in pieces(c):
+                nc.scalar.activation(root[:, :, part], den[c][:, :, part], ACT.Abs_reciprocal_sqrt, scale=0.5)
+            for part in pieces(c):
+                nc.scalar.activation(inv[c][:, :, part], root[:, :, part], ACT.Square)
 
         def finish(c):
             cols = slice(c * OW, (c + 1) * OW)
             y = tile(f"y_{c}", [P, PACK, OW], F32)
-            nc.vector.tensor_tensor(y[:], num[c][:], inv[c][:], ALU.mult)
+            for part in pieces(c):
+                nc.vector.tensor_tensor(y[:, :, part], num[c][:, :, part], inv[c][:, :, part], ALU.mult)
             nc.sync.dma_start(out_rows[:, :, cols], y[:])
             y_packed = tile(f"y_packed_{c}", [P, OW, PACK], BF16)
-            nc.vector.tensor_copy(y_packed[:], y[:].rearrange("p t j -> p j t"))
-            nc.vector.quantize_mx(
-                out=y_codes[:, cols].bitcast(FP8X4), scales=y_scales[:, cols], in_=y_packed[:].rearrange("p j t -> p (j t)")
-            )
+            round_copy = nc.scalar.copy if c == chunks - 2 else nc.vector.tensor_copy
+            for part in pieces(c):
+                round_copy(y_packed[:, part, :], y[:, :, part].rearrange("p t j -> p j t"))
+            for part in pieces(c):
+                place = slice(c * OW + part.start, c * OW + part.stop)
+                nc.vector.quantize_mx(
+                    out=y_codes[:, place].bitcast(FP8X4), scales=y_scales[:, place],
+                    in_=y_packed[:, part, :].rearrange("p j t -> p (j t)"),
+                )
             nc.sync.dma_start(out_words[:, cols], y_codes[:, cols].bitcast(I32))
 
         for k in range(chunks + 3):

@@ -47,24 +47,24 @@ def tile_picked_twksjointbharm_none_po_kernel(
 
         d_bytes = tile("d_bytes", [P, T], U8)
         x_bytes = tile("x_bytes", [P, T], U8)
-        key_scales = tile("key_scales", [P, S], U8)
+        placed = tile("placed", [P, 2 * S], U8)
+        idx_scales = tile("idx_scales", [P, S], U8)
         w_bytes = tile("w_bytes", [P, S], U8)
         nc.vector.memset(d_bytes[:].bitcast(I32), 0)
         nc.gpsimd.memset(x_bytes[:, : T // 2].bitcast(I32), 0)
         nc.vector.memset(x_bytes[:, T // 2 :].bitcast(I32), 0)
-        nc.vector.memset(key_scales[:].bitcast(I32), 0)
-        nc.vector.memset(w_bytes[:].bitcast(I32), 0)
-
-        def load_scale_rows(dst, src):
-            for q in range(4):
-                nc.sync.dma_start(dst[32 * q : 32 * q + 4, :].bitcast(I32), src[0, 4 * q : 4 * q + 4, :].bitcast(I32))
+        for t in (placed, idx_scales, w_bytes):
+            nc.vector.memset(t[:].bitcast(I32), 0)
 
         k1_t = load_list("k1_t", k1)
         two_t = load_list("two_t", two)
         nc.sync.dma_start(d_bytes[0:P:8, :].bitcast(I32), d_scales[0].bitcast(I32))
+        nc.sync.dma_start(x_bytes[0:P:8, :].bitcast(I32), x_scales[0].bitcast(I32))
         d_table = tile("d_table", [P, T], U32)
         nc.sync.dma_start(d_table[:].bitcast(I32), words_view(d_words))
-        load_scale_rows(x_bytes, x_scales)
+        n1_t = load_list("n1_t", n1)
+        n2_t = load_list("n2_t", n2)
+        n3_t = load_list("n3_t", n3)
         x_table = tile("x_table", [P, T], U32)
         nc.sync.dma_start(x_table[:].bitcast(I32), words_view(x_words))
 
@@ -77,18 +77,19 @@ def tile_picked_twksjointbharm_none_po_kernel(
 
         key_bytes = tile("key_bytes", [P, S], U8)
         nc.vector.tensor_copy(key_bytes[:], d_bytes[:].indirect(k1_t[:]))
-        staged = tile("staged", [P, S], U8)
-        deal(nc.vector.tensor_copy, staged[:], key_bytes[:])
-        place_rows(nc.sync, key_scales, staged)
+        staged = tile("staged", [P, 2 * S], U8)
+        deal(nc.vector.tensor_copy, staged[:, :S], key_bytes[:])
+        two_bytes = tile("two_bytes", [P, S], U8)
+        nc.vector.tensor_copy(two_bytes[:], x_bytes[:].indirect(two_t[:]))
+        nc.vector.tensor_copy(staged[:, S:].bitcast(I32), two_bytes[:].bitcast(I32))
+        place_rows(nc.sync, placed, staged)
         offs_t = load_list("offs_t", offs)
-        n1_t = load_list("n1_t", n1)
-        n2_t = load_list("n2_t", n2)
         gain = tile("gain", [P, PACK], F32)
         nc.sync.dma_start(gain[:], gn.rearrange("(p t) o -> p (t o)", t=PACK))
         w_raw = tile("w_raw", [P, 2 * S], U8)
         nc.sync.dma_start(w_raw[:].bitcast(I32), w1_words[0].bitcast(I32))
-        load_scale_rows(w_bytes, w1_scales)
-        n3_t = load_list("n3_t", n3)
+        for q in range(4):
+            nc.sync.dma_start(w_bytes[32 * q : 32 * q + 4, :].bitcast(I32), w1_scales[0, 4 * q : 4 * q + 4, :].bitcast(I32))
         key_codes = tile("key_codes", [P, S], U32)
         dealt_codes = key_codes[:].rearrange("p (t m) -> p m t", t=PACK)
         key_words = []
@@ -97,8 +98,6 @@ def tile_picked_twksjointbharm_none_po_kernel(
             nc.vector.tensor_copy(key_words[u][:], d_table[:].indirect(entries(k1_t, u * S // 2, S // 2)))
         for u in range(2):
             nc.vector.tensor_copy(dealt_codes[:, u * P // 2 : (u + 1) * P // 2, :], key_words[u][:].rearrange("p (m t) -> p m t", t=PACK))
-        two_scales = tile("two_scales", [P, S], U8)
-        nc.vector.tensor_copy(two_scales[:], x_bytes[:].indirect(two_t[:]))
         two_codes = keep.tile([P, S], U32, name="two_codes", tag="word_stage_0", align_bytes=64)
         nc.vector.tensor_copy(two_codes[:], x_table[:].indirect(two_t[:]))
 
@@ -108,18 +107,19 @@ def tile_picked_twksjointbharm_none_po_kernel(
                 bank = psum.tile([P, S], F32, name=f"{name}{t}")
                 cols = slice(P * t, P * (t + 1))
                 nc.tensor.matmul_mx(
-                    out=bank[:], lhsT=key_codes[:, cols].bitcast(FP8X4), lhsT_scale=key_scales[:, cols],
+                    out=bank[:], lhsT=key_codes[:, cols].bitcast(FP8X4), lhsT_scale=placed[:, cols],
                     rhs=codes[:].bitcast(FP8X4), rhs_scale=scales, start=True, stop=True,
                 )
                 banks.append(bank)
             return banks
 
-        b_banks = score("bh", two_codes, two_scales[:])
+        b_banks = score("bh", two_codes, placed[:, S:])
 
+        idx_bytes = tile("idx_bytes", [P, S], U8)
+        nc.vector.tensor_copy(idx_bytes[:], x_bytes[:].indirect(offs_t[:]))
+        place_rows(nc.sync, idx_scales, idx_bytes)
         idx_codes = keep.tile([P, S], U32, name="idx_codes", tag="word_stage_1", align_bytes=64)
         nc.vector.tensor_copy(idx_codes[:], x_table[:].indirect(offs_t[:]))
-        idx_scales = tile("idx_scales", [P, S], U8)
-        nc.vector.tensor_copy(idx_scales[:], x_bytes[:].indirect(offs_t[:]))
         a_banks = score("a", idx_codes, idx_scales[:])
 
         gain16 = tile("gain16", [P, PACK], F32)

from contextlib import ExitStack

import concourse.mybir as mybir

F32 = mybir.dt.float32
BF16 = mybir.dt.bfloat16
I32 = mybir.dt.int32
U32 = mybir.dt.uint32
U16 = mybir.dt.uint16
U8 = mybir.dt.uint8
FP8X4 = mybir.dt.float8_e4m3fn_x4
FP4X4 = mybir.dt.float4_e2m1fn_x4
ACT = mybir.ActivationFunctionType
ALU = mybir.AluOpType

P = 128
PACK = 4
T = 2048
S = 512
ZW = 256
OW = 128
ON_VECTOR = (2, 2, 3, 3)
FLOPS = 3 * 2 * 512 * 512 * 512


def tile_picked_twksjointbharm_none_po_kernel(
    tc, x_words, x_scales, d_words, d_scales, gn, w1_words, w1_scales, offs, k1, two, n1, n2, n3, out_0, out_1, out_2
):
    nc = tc.nc
    with ExitStack() as ctx:
        keep = ctx.enter_context(tc.tile_pool(name="keep", bufs=1))
        psum = ctx.enter_context(tc.psum_pool(name="psum", bufs=1))

        def tile(name, shape, dtype):
            return keep.tile(shape, dtype, name=name, align_bytes=64)

        def load_list(name, src):
            t = tile(name, [P, S // 16], U16)
            nc.sync.dma_start(t[:], src)
            return t

        def words_view(src):
            return src[0].rearrange("p n r -> p (n r)").bitcast(I32)

        def entries(lst, start, count):
            return lst[:, start // 16 : (start + count) // 16]

        d_bytes = tile("d_bytes", [P, T], U8)
        x_bytes = tile("x_bytes", [P, T], U8)
        placed = tile("placed", [P, 2 * S], U8)
        idx_scales = tile("idx_scales", [P, S], U8)
        w_bytes = tile("w_bytes", [P, S], U8)
        nc.vector.memset(d_bytes[:].bitcast(I32), 0)
        nc.gpsimd.memset(x_bytes[:, : T // 2].bitcast(I32), 0)
        nc.vector.memset(x_bytes[:, T // 2 :].bitcast(I32), 0)
        for t in (placed, idx_scales, w_bytes):
            nc.vector.memset(t[:].bitcast(I32), 0)

        k1_t = load_list("k1_t", k1)
        two_t = load_list("two_t", two)
        nc.sync.dma_start(d_bytes[0:P:8, :].bitcast(I32), d_scales[0].bitcast(I32))
        nc.sync.dma_start(x_bytes[0:P:8, :].bitcast(I32), x_scales[0].bitcast(I32))
        d_table = tile("d_table", [P, T], U32)
        nc.sync.dma_start(d_table[:].bitcast(I32), words_view(d_words))
        n1_t = load_list("n1_t", n1)
        n2_t = load_list("n2_t", n2)
        n3_t = load_list("n3_t", n3)
        x_table = tile("x_table", [P, T], U32)
        nc.sync.dma_start(x_table[:].bitcast(I32), words_view(x_words))

        def deal(engine_copy, dst, src):
            engine_copy(dst.rearrange("p (t m) -> p m t", t=PACK), src.rearrange("p (m t) -> p m t", t=PACK))

        def place_rows(queue, dst, src):
            for r in range(4):
                queue.dma_start(dst[r:P:32, :].bitcast(I32), src[8 * r : P : 32, :].bitcast(I32))

        key_bytes = tile("key_bytes", [P, S], U8)
        nc.vector.tensor_copy(key_bytes[:], d_bytes[:].indirect(k1_t[:]))
        staged = tile("staged", [P, 2 * S], U8)
        deal(nc.vector.tensor_copy, staged[:, :S], key_bytes[:])
        two_bytes = tile("two_bytes", [P, S], U8)
        nc.vector.tensor_copy(two_bytes[:], x_bytes[:].indirect(two_t[:]))
        nc.vector.tensor_copy(staged[:, S:].bitcast(I32), two_bytes[:].bitcast(I32))
        place_rows(nc.sync, placed, staged)
        offs_t = load_list("offs_t", offs)
        gain = tile("gain", [P, PACK], F32)
        nc.sync.dma_start(gain[:], gn.rearrange("(p t) o -> p (t o)", t=PACK))
        w_raw = tile("w_raw", [P, 2 * S], U8)
        nc.sync.dma_start(w_raw[:].bitcast(I32), w1_words[0].bitcast(I32))
        for q in range(4):
            nc.sync.dma_start(w_bytes[32 * q : 32 * q + 4, :].bitcast(I32), w1_scales[0, 4 * q : 4 * q + 4, :].bitcast(I32))
        key_codes = tile("key_codes", [P, S], U32)
        dealt_codes = key_codes[:].rearrange("p (t m) -> p m t", t=PACK)
        key_words = []
        for u in range(2):
            key_words.append(keep.tile([P, S // 2], U32, name=f"key_words_{u}", tag=f"word_stage_{u}", align_bytes=64))
            nc.vector.tensor_copy(key_words[u][:], d_table[:].indirect(entries(k1_t, u * S // 2, S // 2)))
        for u in range(2):
            nc.vector.tensor_copy(dealt_codes[:, u * P // 2 : (u + 1) * P // 2, :], key_words[u][:].rearrange("p (m t) -> p m t", t=PACK))
        two_codes = keep.tile([P, S], U32, name="two_codes", tag="word_stage_0", align_bytes=64)
        nc.vector.tensor_copy(two_codes[:], x_table[:].indirect(two_t[:]))

        def score(name, codes, scales):
            banks = []
            for t in range(PACK):
                bank = psum.tile([P, S], F32, name=f"{name}{t}")
                cols = slice(P * t, P * (t + 1))
                nc.tensor.matmul_mx(
                    out=bank[:], lhsT=key_codes[:, cols].bitcast(FP8X4), lhsT_scale=placed[:, cols],
                    rhs=codes[:].bitcast(FP8X4), rhs_scale=scales, start=True, stop=True,
                )
                banks.append(bank)
            return banks

        b_banks = score("bh", two_codes, placed[:, S:])

        idx_bytes = tile("idx_bytes", [P, S], U8)
        nc.vector.tensor_copy(idx_bytes[:], x_bytes[:].indirect(offs_t[:]))
        place_rows(nc.sync, idx_scales, idx_bytes)
        idx_codes = keep.tile([P, S], U32, name="idx_codes", tag="word_stage_1", align_bytes=64)
        nc.vector.tensor_copy(idx_codes[:], x_table[:].indirect(offs_t[:]))
        a_banks = score("a", idx_codes, idx_scales[:])

        gain16 = tile("gain16", [P, PACK], F32)
        nc.gpsimd.tensor_scalar(gain16[:], gain[:], 0.0625, 0.0, ALU.mult, ALU.add)
        w_codes = tile("w_codes", [P, 2 * S], U8)
        deal(nc.scalar.copy, w_codes[:].bitcast(U16), w_raw[:].bitcast(U16))
        w_scales = tile("w_scales", [P, S], U8)
        deal(nc.vector.tensor_copy, w_scales[:], w_bytes[:])

        b_rows = [tile(f"b_row{t}", [P, S], F32) for t in range(PACK)]
        h_rows = [tile(f"h_row{t}", [P, S], F32) for t in range(PACK)]
        h_sq = {}
        halves = S // ZW
        b1 = [tile(f"b1_{c}", [P, PACK, ZW], F32) for c in range(halves)]
        diff = [tile(f"diff_{c}", [P, PACK, ZW], F32) for c in range(halves)]
        th = [tile(f"th_{c}", [P, PACK, ZW], F32) for c in range(halves)]
        z_rows = [tile(f"z_rows_{c}", [P, PACK, ZW], BF16) for c in range(halves)]
        h_banks = {}

        def fetch_b(c, t):
            if c == 0:
                copy_out = nc.vector.tensor_copy if t == PACK - 1 else nc.scalar.copy
                copy_out(b_rows[t][:], b_banks[t][:])
            nc.scalar.activation(b1[c][:, t, :], b_rows[t][:].indirect(entries(n1_t, c * ZW, ZW)), ACT.Copy)
            at_n2 = b_rows[t][:].indirect(entries(n2_t, c * ZW, ZW))
            nc.vector.tensor_tensor(diff[c][:, t, :], at_n2, b1[c][:, t, :], ALU.subtract)

        def make_z(c, t):
            nc.scalar.activation(th[c][:, t, :], diff[c][:, t, :], ACT.Tanh, scale=-0.0625)
            nc.vector.scalar_tensor_tensor(
                z_rows[c][:, t, :], a_banks[t][:, c * ZW : (c + 1) * ZW], gain16[:, t : t + 1], th[c][:, t, :], ALU.mult, ALU.mult
            )

        def layer(c):
            cols = slice(c * ZW, (c + 1) * ZW)
            z_packed = keep.tile([P, ZW, PACK], BF16, name=f"z_packed_{c}", tag=f"packed_{c}", align_bytes=64)
            nc.vector.tensor_copy(z_packed[:], z_rows[c][:].rearrange("p t j -> p j t"))
            z_codes = tile(f"z_codes_{c}", [P, ZW], U32)
            z_scales = tile(f"z_scales_{c}", [P, ZW], U8)
            nc.vector.quantize_mx(out=z_codes[:].bitcast(FP8X4), scales=z_scales[:], in_=z_packed[:].rearrange("p j t -> p (j t)"))
            for u in range(2):
                h_banks[c, u] = psum.tile([P, 2, ZW], F32, name=f"bh{2 * c + u}")
            for t in range(PACK):
                nc.tensor.matmul_mx(
                    out=h_banks[c, t // 2][:, t % 2, :], lhsT=w_codes[:, 2 * P * t : 2 * P * (t + 1)].bitcast(FP4X4),
                    lhsT_scale=w_scales[:, P * t : P * (t + 1)],
                    rhs=z_codes[:].bitcast(FP8X4), rhs_scale=z_scales[:], start=True, stop=True,
                )
            for t in range(PACK):
                nc.scalar.copy(h_rows[t][:, cols], h_banks[c, t // 2][:, t % 2, :])

        steps = sorted(((c, t) for c in range(halves) for t in range(PACK)), key=lambda s: (2 * s[1] + 3 * s[0], s[0]))
        for k in range(len(steps) + 2):
            if k < len(steps):
                fetch_b(*steps[k])
            if k >= 2:
                c, t = steps[k - 2]
                make_z(c, t)
                if k == len(steps) + 1:
                    warm = tile("warm", [P, 1], F32)
                    nc.scalar.activation(warm[:], th[c][:, t, 0:1], ACT.Abs_reciprocal_sqrt, bias=2.0)
                if t == PACK - 1:
                    layer(c)
        h_sq[0] = keep.tile([P, PACK, ZW], F32, name="h_sq_0", tag="packed_1", align_bytes=64)
        for t in range(PACK):
            nc.vector.tensor_tensor(h_sq[0][:, t, :], h_rows[t][:, :ZW], h_rows[t][:, :ZW], ALU.mult)

        def square_second_half():
            h_sq[1] = tile("h_sq_1", [P, PACK, ZW], F32)
            for u in range(2):
                nc.scalar.activation(h_sq[1][:, 2 * u : 2 * u + 2, :], h_banks[1, u][:], ACT.Square)

        y_codes = tile("y_codes", [P, S], U32)
        y_scales = tile("y_scales", [P, S], U8)
        out_rows = out_0.rearrange("(p t) j -> p t j", t=PACK)
        out_words = words_view(out_1)
        chunks = S // OW
        pa = [tile(f"pa_{c}", [P, PACK, OW], F32) for c in range(chunks)]
        pa_sq = [tile(f"pa_sq_{c}", [P, PACK, OW], F32) for c in range(chunks)]
        num = [tile(f"num_{c}", [P, PACK, OW], F32) for c in range(chunks)]
        den = [tile(f"den_{c}", [P, PACK, OW], F32) for c in range(chunks)]
        inv = [tile(f"inv_{c}", [P, PACK, OW], F32) for c in range(chunks)]

        def fetch_h(c):
            for t in range(PACK):
                looked_up = h_rows[t][:].indirect(entries(n3_t, c * OW, OW))
                if t < ON_VECTOR[c]:
                    nc.vector.tensor_copy(pa[c][:, t, :], looked_up)
                else:
                    nc.scalar.activation(pa[c][:, t, :], looked_up, ACT.Copy)
            nc.scalar.activation(pa_sq[c][:], pa[c][:], ACT.Square)

        def sums(c):
            half, start = divmod(c * OW, ZW)
            cols = slice(start, start + OW)
            nc.vector.scalar_tensor_tensor(den[c][:], pa_sq[c][:], 0.5, h_sq[half][:, :, cols], ALU.add, ALU.add)
            for u in range(2):
                pair = slice(2 * u, 2 * u + 2)
                nc.vector.tensor_tensor(num[c][:, pair, :], h_banks[half, u][:, :, cols], pa[c][:, pair, :], ALU.mult)

        def pieces(c):
            count = 2 if c >= chunks - 2 else 1
            return [slice(i * OW // count, (i + 1) * OW // count) for i in range(count)]

        def invert(c):
            root = tile(f"root_{c}", [P, PACK, OW], F32)
            for part in pieces(c):
                nc.scalar.activation(root[:, :, part], den[c][:, :, part], ACT.Abs_reciprocal_sqrt, scale=0.5)
            for part in pieces(c):
                nc.scalar.activation(inv[c][:, :, part], root[:, :, part], ACT.Square)

        def finish(c):
            cols = slice(c * OW, (c + 1) * OW)
            y = tile(f"y_{c}", [P, PACK, OW], F32)
            for part in pieces(c):
                nc.vector.tensor_tensor(y[:, :, part], num[c][:, :, part], inv[c][:, :, part], ALU.mult)
            nc.sync.dma_start(out_rows[:, :, cols], y[:])
            y_packed = tile(f"y_packed_{c}", [P, OW, PACK], BF16)
            round_copy = nc.scalar.copy if c == chunks - 2 else nc.vector.tensor_copy
            for part in pieces(c):
                round_copy(y_packed[:, part, :], y[:, :, part].rearrange("p t j -> p j t"))
            for part in pieces(c):
                place = slice(c * OW + part.start, c * OW + part.stop)
                nc.vector.quantize_mx(
                    out=y_codes[:, place].bitcast(FP8X4), scales=y_scales[:, place],
                    in_=y_packed[:, part, :].rearrange("p j t -> p (j t)"),
                )
            nc.sync.dma_start(out_words[:, cols], y_codes[:, cols].bitcast(I32))

        for k in range(chunks + 3):
            if k < chunks:
                fetch_h(k)
            if k == 2:
                square_second_half()
            if 0 <= k - 1 < chunks:
                sums(k - 1)
            if 0 <= k - 2 < chunks:
                invert(k - 2)
            if 0 <= k - 3 < chunks:
                finish(k - 3)
        for q in range(4):
            queue = nc.sync if q % 2 == 0 else nc.scalar
            queue.dma_start(out_2[0, 4 * q : 4 * q + 4, :].bitcast(I32), y_scales[32 * q : 32 * q + 4, :].bitcast(I32))
